import numpy as np
import ml_dtypes


def mxq(x, axis, fmt="e4m3"):
    dtype, down = {"e4m3": (ml_dtypes.float8_e4m3fn, 7), "e5m2": (ml_dtypes.float8_e5m2, 14)}[fmt]
    v = np.moveaxis(np.asarray(x, np.float32).astype(ml_dtypes.bfloat16).astype(np.float64), axis, -1)
    blocks = v.reshape(v.shape[:-1] + (-1, 32))
    amax = np.abs(blocks).max(-1, keepdims=True)
    byte = np.maximum(np.where(amax > 0, np.frexp(amax)[1] - 1 + 127, 0) - down, 1)
    scale = np.exp2(byte - 127.0)
    codes = (blocks / scale).astype(np.float32).astype(dtype).astype(np.float64)
    return np.moveaxis((codes * scale).reshape(v.shape), -1, axis)


WIDE = False


def mx_kscale(k):
    if not WIDE:
        return np.ones(k)
    levels = np.array([10, -10, 5, -5, 0])
    if k % 512:
        return np.exp2(np.random.permutation(np.resize(levels, k // 32))).repeat(32)
    a = np.empty((k // 512, 16))
    for p in range(k // 512):
        a[p, :8] = np.random.permutation(np.resize(levels, 8))
        for g in range(8):
            far = levels[np.abs(levels - a[p, g]) >= 10]
            a[p, g + 8] = far[np.random.randint(len(far))]
    return np.exp2(a.ravel()).repeat(32)


BF16 = ml_dtypes.bfloat16


def bf(x):
    return np.asarray(x, np.float32).astype(BF16)


def f64(x):
    return np.asarray(x).astype(np.float64)

def planes(Y):
    n, m = Y.shape
    b = f64(bf(Y)).reshape(n // 32, 32, m)
    amax = np.abs(b).max(1)
    byte = np.clip(np.where(amax > 0, np.frexp(amax)[1] - 1 + 127 - 7, 1), 1, 254)
    codes = (b * np.exp2(127.0 - byte)[:, None, :]).reshape(n, m).astype(np.float32).astype(ml_dtypes.float8_e4m3fn).view(np.uint8)
    words = codes.reshape(n // 512, 128, 4, m).transpose(0, 1, 3, 2)
    return np.ascontiguousarray(words), np.ascontiguousarray(byte.astype(np.uint8).reshape(n // 512, 16, m))


H, N, M, D = 4, 1024, 512, 512


def biased_softmax(scores, bias):
    z = scores + bias[:, None, :]
    z = z - np.max(z, axis=-1, keepdims=True)
    e = np.exp(z)
    return e / np.sum(e, axis=-1, keepdims=True)


def setup_inputs():
    s, t = mx_kscale(M), mx_kscale(N)
    return {
        "s_ref": bf(np.random.standard_normal((H, N, M)) * 2.0),
        "beta": bf(np.random.standard_normal((H, M)) * 0.5),
        "v_cmp": bf(np.random.standard_normal((H, M, D)) / s[None, :, None]),
        "g_val": bf(np.random.standard_normal((H, M)) * s[None, :]),
        "y_ref": bf(np.random.standard_normal((H, N, D)) * 0.5),
        "a_res": bf((1.0 + 0.1 * np.random.standard_normal((H, N))) / t[None, :]),
        "w_ref": bf(np.random.standard_normal((H, N)) * (np.sqrt(N) / 8.0) * t[None, :]),
    }


def core(s_ref, beta, v_cmp, g_val, y_ref, a_res, w_ref):
    v, g, a, w = f64(v_cmp), f64(g_val), f64(a_res), f64(w_ref)

    p = biased_softmax(f64(s_ref), f64(beta))

    pg = p * g[:, None, :]
    r = a[:, :, None] * ((mxq(pg, 2, "e4m3") @ mxq(v, 1, "e4m3")) - f64(y_ref))

    pw = p * w[:, :, None]
    grad = mxq(pw.transpose(0, 2, 1), 2, "e4m3") @ mxq(r, 1, "e4m3")

    c = np.sum(p, axis=1)

    return g[:, :, None] * v - 2.0 * grad / (c[:, :, None] + 0.5)


def reference(s_ref, beta, v_cmp, g_val, y_ref, a_res, w_ref):
    R_out = core(s_ref, beta, v_cmp, g_val, y_ref, a_res, w_ref)
    words, scales = planes(np.moveaxis(R_out, 1, 0).reshape(512, -1))
    return R_out, words, scales

@@ -1,0 +1,383 @@
+from contextlib import ExitStack
+
+import concourse.mybir as mybir
+from concourse.masks import make_identity
+
+H, N, M, D = 4, 1024, 512, 512
+P = 128
+G = 2 * H
+FLOPS = 2 * 2 * H * N * M * D
+
+F32 = mybir.dt.float32
+BF16 = mybir.dt.bfloat16
+U32 = mybir.dt.uint32
+I32 = mybir.dt.int32
+U8 = mybir.dt.uint8
+FP8X4 = mybir.dt.float8_e4m3fn_x4
+ACT = mybir.ActivationFunctionType
+ALU = mybir.AluOpType
+AX = mybir.AxisListType
+
+
+def tile_masspreconditionedvaluegradientstep_kernel(
+    tc, s_ref, beta, v_cmp, g_val, y_ref, a_res, w_ref, out_0, out_1, out_2
+):
+    nc = tc.nc
+    with ExitStack() as ctx:
+        const = ctx.enter_context(tc.tile_pool(name="const", bufs=1))
+        sb = ctx.enter_context(tc.tile_pool(name="sb", bufs=2))
+        psum = ctx.enter_context(tc.psum_pool(name="psum", bufs=1))
+        ctx.enter_context(tc.manual_schedule())
+
+        s_sb, y_sb, v_sb = {}, {}, {}
+
+        def load_s(g):
+            t = sb.tile([P, 4, M], BF16, name="s_sb", tag="s_sb", bufs=5, align_bytes=64)
+            h, gg = divmod(g, 2)
+            nc.sync.dma_start(out=t[:], in_=s_ref[h, 512 * gg : 512 * gg + 512, :].rearrange("(p j) m -> p j m", j=4))
+            s_sb[g] = t
+
+        def load_y(g):
+            t = sb.tile([P, 4, D], BF16, name="y_sb", tag="y_sb", bufs=4, align_bytes=64)
+            h, gg = divmod(g, 2)
+            nc.sync.dma_start(out=t[:], in_=y_ref[h, 512 * gg : 512 * gg + 512, :].rearrange("(p j) d -> p j d", j=4))
+            y_sb[g] = t
+
+        def load_v(h):
+            t = sb.tile([P, 4, D], BF16, name="v_sb", tag="v_sb", bufs=2, align_bytes=64)
+            nc.sync.dma_start(out=t[:], in_=v_cmp[h].rearrange("(p j) d -> p j d", j=4))
+            v_sb[h] = t
+
+        warm = const.tile([P, 1], F32, name="warm")
+        nc.vector.memset(warm[:], 0.0)
+        nc.scalar.activation(out=warm[:], in_=warm[:], func=ACT.Exp)
+
+        load_s(0)
+        braw = const.tile([P, P], BF16, name="braw")
+        nc.vector.memset(braw[:], 0.0)
+        nc.scalar.dma_start(out=braw[0:16, :], in_=beta.rearrange("h (b k) -> (h b) k", k=P))
+        beta_b = const.tile([P, H * M], BF16, name="beta_b")
+        g_raw = const.tile([P, H * M], BF16, name="g_raw")
+        a_bf = const.tile([P, H, 2, 4], BF16, name="a_bf")
+        w_bf = const.tile([P, H, 2, 4], BF16, name="w_bf")
+        gt_bf = const.tile([P, H, 4], BF16, name="gt_bf")
+        nc.scalar.dma_start(out=beta_b[:], in_=beta.rearrange("h m -> (h m)").partition_broadcast(P))
+        nc.scalar.dma_start(out=g_raw[:], in_=g_val.rearrange("h m -> (h m)").partition_broadcast(P))
+        nc.scalar.dma_start(out=w_bf[:], in_=w_ref.rearrange("h (g p j) -> p h g j", g=2, j=4))
+        nc.scalar.dma_start(out=a_bf[:], in_=a_res.rearrange("h (g p j) -> p h g j", g=2, j=4))
+        nc.scalar.dma_start(out=gt_bf[:], in_=g_val.rearrange("h (p t) -> p h t", t=4))
+        load_v(0)
+        load_s(1)
+        load_y(0)
+        load_s(2)
+        load_y(1)
+
+        ident_b = const.tile([P, P], BF16, name="ident_b")
+        make_identity(nc, ident_b[:])
+        ident_f = const.tile([P, P], F32, name="ident_f")
+        make_identity(nc, ident_f[:])
+
+        bt_ps = psum.tile([P, P], BF16, name="bt_ps", tag="xt", bufs=1)
+        nc.tensor.transpose(bt_ps[:], braw[:], ident_b[:])
+        beta_t = const.tile([P, 16], F32, name="beta_t")
+        nc.vector.tensor_copy(out=beta_t[:], in_=bt_ps[:, 0:16])
+        a_f = const.tile([P, 32], F32, name="a_f")
+        nc.vector.tensor_copy(out=a_f[:], in_=a_bf[:].rearrange("p h g j -> p (h g j)"))
+        w_f = const.tile([P, 32], F32, name="w_f")
+        nc.vector.tensor_copy(out=w_f[:], in_=w_bf[:].rearrange("p h g j -> p (h g j)"))
+        gt_f = const.tile([P, 16], F32, name="gt_f")
+        nc.vector.tensor_copy(out=gt_f[:], in_=gt_bf[:].rearrange("p h t -> p (h t)"))
+        g_b = const.tile([P, H, M], F32, name="g_b")
+
+        def make_gb(h):
+            src = g_raw[:, M * h : M * h + M].rearrange("p (q u e) -> p u q e", u=2, e=2)
+            dst = g_b[:, h, :].rearrange("p (u q e) -> p u q e", u=2, e=2)
+            nc.gpsimd.tensor_scalar(out=dst, in0=src, scalar1=1.0, scalar2=0.0, op0=ALU.mult, op1=ALU.add)
+
+        beta_w = {}
+
+        def make_bw(h):
+            beta_w[h] = sb.tile([P, 4, P], F32, name="beta_w", tag="beta_w", bufs=2, align_bytes=64)
+            nc.vector.tensor_copy(
+                out=beta_w[h][:], in_=beta_t[:, 4 * h : 4 * h + 4].unsqueeze(2).to_broadcast([P, 4, P])
+            )
+
+        make_bw(0)
+        make_gb(0)
+
+        e_t, nmax, den, rden, fac = {}, {}, {}, {}, {}
+        pg, xts, pgt, pgc, pgs = {}, {}, {}, {}, {}
+        pw, pwc, pws = {}, {}, {}
+        u_t, ay_t, r_t, rc, rs = {}, {}, {}, {}, {}
+        vb, vc, vs, gv, kf, cps = {}, {}, {}, {}, {}, {}
+        o_t, ob, oc, osc = {}, {}, {}, {}
+
+        zt = {}
+
+        def z_make(g, j):
+            h = g // 2
+            if j == 0:
+                e_t[g] = sb.tile([P, 4, M], F32, name="e_t", tag="e_t", bufs=2, align_bytes=64)
+                nmax[g] = sb.tile([P, 4], F32, name="nmax", tag="nmax", bufs=3)
+                den[g] = sb.tile([P, 4], F32, name="den", tag="den", bufs=3)
+            if j < 3:
+                z = psum.tile([P, M], F32, name="z_ps", tag="z", bufs=3)
+                nc.tensor.matmul(out=z[:], lhsT=ident_b[:], rhs=s_sb[g][:, j, :], start=True, stop=False)
+                for b in range(4):
+                    nc.tensor.matmul(
+                        out=z[:, P * b : P * b + P],
+                        lhsT=beta_w[h][:, b, :],
+                        rhs=ident_f[:],
+                        start=False,
+                        stop=(b == 3),
+                        is_transpose=True,
+                    )
+            else:
+                z = sb.tile([P, M], F32, name="z_sb", tag="z_sb", bufs=2, align_bytes=64)
+                nc.gpsimd.tensor_tensor(out=z[:], in0=s_sb[g][:, j, :], in1=beta_b[:, M * h : M * h + M], op=ALU.add)
+            zt[g, j] = z
+
+        def z_max(g, j):
+            nc.vector.tensor_reduce(out=nmax[g][:, j : j + 1], in_=zt[g, j][:], axis=AX.X, op=ALU.max, negate=True)
+
+        def z_exp(g, j):
+            z = zt[g, j]
+            nc.scalar.activation(
+                out=e_t[g][:, j, :].rearrange("p (u q e) -> p u q e", u=2, e=2),
+                in_=z[:].rearrange("p (q u e) -> p u q e", u=2, e=2),
+                func=ACT.Exp,
+                bias=nmax[g][:, j : j + 1],
+                scale=1.0,
+                accum_out=den[g][:, j : j + 1],
+            )
+
+        def recips(g):
+            rden[g] = sb.tile([P, 4], F32, name="rden", tag="rden", bufs=3)
+            fac[g] = sb.tile([P, 4], F32, name="fac", tag="fac", bufs=3)
+            nc.vector.reciprocal(out=rden[g][:], in_=den[g][:])
+            nc.vector.tensor_tensor(out=fac[g][:], in0=rden[g][:], in1=w_f[:, 4 * g : 4 * g + 4], op=ALU.mult)
+
+        def pg_mul(g, j):
+            if j == 0:
+                pg[g] = sb.tile([P, 4, M], BF16, name="pg", tag="pg", bufs=2, align_bytes=64)
+            nc.vector.scalar_tensor_tensor(
+                out=pg[g][:, j, :], in0=e_t[g][:, j, :], scalar=rden[g][:, j : j + 1], in1=g_b[:, g // 2, :],
+                op0=ALU.mult, op1=ALU.mult,
+            )
+
+        def pg_turn(g, jp):
+            xt = psum.tile([P, 2, 2, P], F32, name="xt", tag="xt", bufs=1)
+            for jj in range(2):
+                for u in range(2):
+                    nc.tensor.transpose(
+                        xt[:, jj, u, :], pg[g][:, 2 * jp + jj, 256 * u : 256 * u + 256].bitcast(F32), ident_f[:]
+                    )
+            if jp == 0:
+                pgt[g] = sb.tile([P, 4 * P, 4], BF16, name="pgt", tag="pgt", bufs=2, align_bytes=64)
+            dst = pgt[g][:, 256 * jp : 256 * jp + 256, :].rearrange("p n t -> p (n t)").bitcast(F32)
+            nc.scalar.copy(
+                out=dst.rearrange("p (j n u) -> p j n u", j=2, u=2),
+                in_=xt[:].rearrange("p j u n -> p j n u"),
+            )
+
+        def quant(src, tag, bufs):
+            codes = sb.tile([P, 512], U32, name=tag + "_c", tag=tag + "_c", bufs=bufs, align_bytes=64)
+            scales = sb.tile([P, 512], U8, name=tag + "_s", tag=tag + "_s", bufs=bufs, align_bytes=64)
+            nc.vector.quantize_mx(
+                out=codes[:].bitcast(FP8X4), scales=scales[:], in_=src[:].rearrange("p c j -> p (c j)")
+            )
+            return codes, scales
+
+        def pw_mul(g, u):
+            if u == 0:
+                pw[g] = sb.tile([P, M, 4], BF16, name="pw", tag="pw", bufs=2, align_bytes=64)
+            nc.vector.tensor_tensor(
+                out=pw[g][:, 256 * u : 256 * u + 256, :].rearrange("p (e q) j -> p q e j", e=2),
+                in0=e_t[g][:, :, 256 * u : 256 * u + 256].rearrange("p j (q e) -> p q e j", e=2),
+                in1=fac[g][:].unsqueeze(1).unsqueeze(1).to_broadcast([P, P, 2, 4]),
+                op=ALU.mult,
+            )
+
+        cpart = {}
+
+        def mass(g):
+            ps = psum.tile([P, 16], F32, name="cps", tag="xt", bufs=1)
+            for t in range(4):
+                u, e = divmod(t, 2)
+                for j in range(4):
+                    nc.tensor.matmul(
+                        out=ps[:, 4 * t + j : 4 * t + j + 1],
+                        lhsT=e_t[g][:, j, 256 * u + e : 256 * u + 256 : 2],
+                        rhs=rden[g][:, j : j + 1],
+                        start=True,
+                        stop=True,
+                    )
+            cps[g] = ps
+
+        def mass_sum(g):
+            cpart[g] = sb.tile([P, 4], F32, name="cpart", tag="cpart", bufs=4)
+            nc.vector.tensor_reduce(
+                out=cpart[g][:], in_=cps[g][:].rearrange("p (t j) -> p t j", t=4), axis=AX.X, op=ALU.add
+            )
+
+        def mass_fac(h):
+            cs = sb.tile([P, 4], F32, name="cs", tag="cs", bufs=2)
+            ch = sb.tile([P, 4], F32, name="ch", tag="ch", bufs=2)
+            kf[h] = sb.tile([P, 4], F32, name="kf", tag="kf", bufs=3)
+            nc.vector.tensor_tensor(out=cs[:], in0=cpart[2 * h][:], in1=cpart[2 * h + 1][:], op=ALU.add)
+            nc.vector.tensor_scalar(out=ch[:], in0=cs[:], scalar1=0.5, scalar2=-0.5, op0=ALU.add, op1=ALU.mult)
+            nc.vector.reciprocal(out=kf[h][:], in_=ch[:])
+
+        def v_lay(h):
+            vb[h] = sb.tile([P, D, 4], BF16, name="vb", tag="vb", bufs=2, align_bytes=64)
+            nc.scalar.copy(
+                out=vb[h][:].rearrange("p (c i) j -> p c j i", i=4),
+                in_=v_sb[h][:].rearrange("p j (c i) -> p c j i", i=4),
+            )
+
+        def v_quant(h):
+            vc[h], vs[h] = quant(vb[h], "vq", 2)
+
+        def gv_make(h):
+            gv[h] = sb.tile([P, 4, D], F32, name="gv", tag="gv", bufs=2, align_bytes=64)
+            for t in range(4):
+                nc.gpsimd.tensor_scalar(
+                    out=gv[h][:, t, :], in0=v_sb[h][:, t, :], scalar1=gt_f[:, 4 * h + t : 4 * h + t + 1], scalar2=0.0,
+                    op0=ALU.mult, op1=ALU.add,
+                )
+
+        def mm1(g, j):
+            h = g // 2
+            acc = psum.tile([P, D], F32, name="acc", tag="acc", bufs=2)
+            nc.tensor.matmul_mx(
+                out=acc[:],
+                lhsT=pgc[g][:, P * j : P * j + P].bitcast(FP8X4),
+                lhsT_scale=pgs[g][:, P * j : P * j + P],
+                rhs=vc[h][:].bitcast(FP8X4),
+                rhs_scale=vs[h][:],
+                start=True,
+                stop=True,
+            )
+            if j == 0:
+                u_t[g] = sb.tile([P, 4, D], F32, name="u_t", tag="u_t", bufs=2, align_bytes=64)
+            nc.scalar.activation(out=u_t[g][:, j, :], in_=acc[:], func=ACT.Copy, scale=a_f[:, 4 * g + j : 4 * g + j + 1])
+
+        def ay_make(g, j):
+            if j == 0:
+                ay_t[g] = sb.tile([P, 4, D], F32, name="ay_t", tag="ay_t", bufs=2, align_bytes=64)
+            nc.scalar.activation(
+                out=ay_t[g][:, j, :], in_=y_sb[g][:, j, :], func=ACT.Copy, scale=a_f[:, 4 * g + j : 4 * g + j + 1]
+            )
+
+        def r_make(g):
+            r_t[g] = sb.tile([P, D, 4], BF16, name="r_t", tag="r_t", bufs=2, align_bytes=64)
+            nc.vector.tensor_tensor(
+                out=r_t[g][:].rearrange("p (c i) j -> p c j i", i=2),
+                in0=u_t[g][:].rearrange("p j (c i) -> p c j i", i=2),
+                in1=ay_t[g][:].rearrange("p j (c i) -> p c j i", i=2),
+                op=ALU.subtract,
+            )
+
+        def finish(h, t):
+            if t == 0:
+                o_t[h] = sb.tile([P, 4, D], F32, name="o_t", tag="o_t", bufs=2, align_bytes=64)
+            gr = psum.tile([P, D], F32, name="gr", tag="gr", bufs=2)
+            for gg in range(2):
+                g = 2 * h + gg
+                nc.tensor.matmul_mx(
+                    out=gr[:],
+                    lhsT=pwc[g][:, P * t : P * t + P].bitcast(FP8X4),
+                    lhsT_scale=pws[g][:, P * t : P * t + P],
+                    rhs=rc[g][:].bitcast(FP8X4),
+                    rhs_scale=rs[g][:],
+                    start=(gg == 0),
+                    stop=(gg == 1),
+                )
+            nc.vector.scalar_tensor_tensor(
+                out=o_t[h][:, t, :], in0=gr[:], scalar=kf[h][:, t : t + 1], in1=gv[h][:, t, :], op0=ALU.mult, op1=ALU.add
+            )
+
+        def store(h):
+            nc.sync.dma_start(out=out_0[h].rearrange("(p t) d -> p t d", t=4), in_=o_t[h][:])
+            ob[h] = sb.tile([P, D, 4], BF16, name="ob", tag="ob", bufs=2, align_bytes=64)
+            nc.scalar.copy(
+                out=ob[h][:].rearrange("p (c i) t -> p c t i", i=2),
+                in_=o_t[h][:].rearrange("p t (c i) -> p c t i", i=2),
+            )
+
+        def store_planes(h):
+            oc[h], osc[h] = quant(ob[h], "oq", 2)
+            cols = slice(D * h, D * h + D)
+            nc.sync.dma_start(
+                out=out_1[0, :, cols, :].rearrange("p m t -> p (m t)").bitcast(I32), in_=oc[h][:].bitcast(I32)
+            )
+            for qq in range(4):
+                nc.sync.dma_start(
+                    out=out_2[0, 4 * qq : 4 * qq + 4, cols].bitcast(I32),
+                    in_=osc[h][32 * qq : 32 * qq + 4, :].bitcast(I32),
+                )
+
+        for i in range(-1, G + 2):
+            gz, gp, gm = i + 1, i, i - 1
+            has_z, has_p, has_m = gz < G, 0 <= gp < G, 0 <= gm < G
+            fh = (i - 3) // 2 if i >= 3 and i % 2 == 1 else None
+            if i >= 0:
+                if i + 3 < G:
+                    load_s(i + 3)
+                if i + 2 < G:
+                    load_y(i + 2)
+                if i % 2 == 0 and i // 2 + 1 < H:
+                    load_v(i // 2 + 1)
+                    make_gb(i // 2 + 1)
+            if has_p:
+                recips(gp)
+            if has_z:
+                for j in range(4):
+                    z_make(gz, j)
+            if has_m:
+                mm1(gm, 0)
+                mm1(gm, 1)
+            for j in range(4):
+                if has_z:
+                    z_max(gz, j)
+                    z_exp(gz, j)
+                if has_p:
+                    pg_mul(gp, j)
+                if has_m and j < 2:
+                    mm1(gm, 2 + j)
+                if fh is not None:
+                    finish(fh, j)
+                if has_p and j % 2 == 1:
+                    pg_turn(gp, j // 2)
+                if j == 1 and has_m:
+                    mass_sum(gm)
+                    if gm % 2 == 1:
+                        mass_fac(gm // 2)
+            if i == -1:
+                v_lay(0)
+                v_quant(0)
+            if has_p:
+                pw_mul(gp, 0)
+                pw_mul(gp, 1)
+            if fh is not None:
+                store(fh)
+            if has_m:
+                r_make(gm)
+            if has_p:
+                pgc[gp], pgs[gp] = quant(pgt[gp], "pgq", 2)
+                mass(gp)
+                pwc[gp], pws[gp] = quant(pw[gp], "pwq", 4)
+                for j in range(4):
+                    ay_make(gp, j)
+            if has_m:
+                rc[gm], rs[gm] = quant(r_t[gm], "rq", 4)
+            if fh is not None:
+                store_planes(fh)
+            if i >= 0 and i % 2 == 1 and (i + 1) // 2 < H:
+                v_lay((i + 1) // 2)
+            if i >= 0 and i % 2 == 0 and i // 2 + 1 < H:
+                make_bw(i // 2 + 1)
+            if has_p and gp % 2 == 0:
+                gv_make(gp // 2)
+                if gp > 0:
+                    v_quant(gp // 2)

@@ -27,7 +27,6 @@ def tile_masspreconditionedvaluegradientstep_kernel(
         const = ctx.enter_context(tc.tile_pool(name="const", bufs=1))
         sb = ctx.enter_context(tc.tile_pool(name="sb", bufs=2))
         psum = ctx.enter_context(tc.psum_pool(name="psum", bufs=1))
-        ctx.enter_context(tc.manual_schedule())
 
         s_sb, y_sb, v_sb = {}, {}, {}
 
@@ -56,13 +55,9 @@ def tile_masspreconditionedvaluegradientstep_kernel(
         braw = const.tile([P, P], BF16, name="braw")
         nc.vector.memset(braw[:], 0.0)
         nc.scalar.dma_start(out=braw[0:16, :], in_=beta.rearrange("h (b k) -> (h b) k", k=P))
-        beta_b = const.tile([P, H * M], BF16, name="beta_b")
-        g_raw = const.tile([P, H * M], BF16, name="g_raw")
         a_bf = const.tile([P, H, 2, 4], BF16, name="a_bf")
         w_bf = const.tile([P, H, 2, 4], BF16, name="w_bf")
         gt_bf = const.tile([P, H, 4], BF16, name="gt_bf")
-        nc.scalar.dma_start(out=beta_b[:], in_=beta.rearrange("h m -> (h m)").partition_broadcast(P))
-        nc.scalar.dma_start(out=g_raw[:], in_=g_val.rearrange("h m -> (h m)").partition_broadcast(P))
         nc.scalar.dma_start(out=w_bf[:], in_=w_ref.rearrange("h (g p j) -> p h g j", g=2, j=4))
         nc.scalar.dma_start(out=a_bf[:], in_=a_res.rearrange("h (g p j) -> p h g j", g=2, j=4))
         nc.scalar.dma_start(out=gt_bf[:], in_=g_val.rearrange("h (p t) -> p h t", t=4))
@@ -77,7 +72,7 @@ def tile_masspreconditionedvaluegradientstep_kernel(
         ident_f = const.tile([P, P], F32, name="ident_f")
         make_identity(nc, ident_f[:])
 
-        bt_ps = psum.tile([P, P], BF16, name="bt_ps", tag="xt", bufs=1)
+        bt_ps = psum.tile([P, P], BF16, name="bt_ps", tag="cps", bufs=1)
         nc.tensor.transpose(bt_ps[:], braw[:], ident_b[:])
         beta_t = const.tile([P, 16], F32, name="beta_t")
         nc.vector.tensor_copy(out=beta_t[:], in_=bt_ps[:, 0:16])
@@ -87,13 +82,6 @@ def tile_masspreconditionedvaluegradientstep_kernel(
         nc.vector.tensor_copy(out=w_f[:], in_=w_bf[:].rearrange("p h g j -> p (h g j)"))
         gt_f = const.tile([P, 16], F32, name="gt_f")
         nc.vector.tensor_copy(out=gt_f[:], in_=gt_bf[:].rearrange("p h t -> p (h t)"))
-        g_b = const.tile([P, H, M], F32, name="g_b")
-
-        def make_gb(h):
-            src = g_raw[:, M * h : M * h + M].rearrange("p (q u e) -> p u q e", u=2, e=2)
-            dst = g_b[:, h, :].rearrange("p (u q e) -> p u q e", u=2, e=2)
-            nc.gpsimd.tensor_scalar(out=dst, in0=src, scalar1=1.0, scalar2=0.0, op0=ALU.mult, op1=ALU.add)
-
         beta_w = {}
 
         def make_bw(h):
@@ -103,10 +91,9 @@ def tile_masspreconditionedvaluegradientstep_kernel(
             )
 
         make_bw(0)
-        make_gb(0)
 
-        e_t, nmax, den, rden, fac = {}, {}, {}, {}, {}
-        pg, xts, pgt, pgc, pgs = {}, {}, {}, {}, {}
+        p_t, nmax, den, rden = {}, {}, {}, {}
+        pgt, pgc, pgs = {}, {}, {}
         pw, pwc, pws = {}, {}, {}
         u_t, ay_t, r_t, rc, rs = {}, {}, {}, {}, {}
         vb, vc, vs, gv, kf, cps = {}, {}, {}, {}, {}, {}
@@ -117,11 +104,11 @@ def tile_masspreconditionedvaluegradientstep_kernel(
         def z_make(g, j):
             h = g // 2
             if j == 0:
-                e_t[g] = sb.tile([P, 4, M], F32, name="e_t", tag="e_t", bufs=2, align_bytes=64)
+                p_t[g] = sb.tile([P, 4, M], F32, name="p_t", tag="p_t", bufs=4, align_bytes=64)
                 nmax[g] = sb.tile([P, 4], F32, name="nmax", tag="nmax", bufs=3)
                 den[g] = sb.tile([P, 4], F32, name="den", tag="den", bufs=3)
             if j < 3:
-                z = psum.tile([P, M], F32, name="z_ps", tag="z", bufs=3)
+                z = psum.tile([P, M], F32, name="z_ps", tag="z", bufs=2)
                 nc.tensor.matmul(out=z[:], lhsT=ident_b[:], rhs=s_sb[g][:, j, :], start=True, stop=False)
                 for b in range(4):
                     nc.tensor.matmul(
@@ -133,8 +120,18 @@ def tile_masspreconditionedvaluegradientstep_kernel(
                         is_transpose=True,
                     )
             else:
-                z = sb.tile([P, M], F32, name="z_sb", tag="z_sb", bufs=2, align_bytes=64)
-                nc.gpsimd.tensor_tensor(out=z[:], in0=s_sb[g][:, j, :], in1=beta_b[:, M * h : M * h + M], op=ALU.add)
+                st = psum.tile([P, 4, P], BF16, name="st_ps", tag="z", bufs=2)
+                for b in range(4):
+                    nc.tensor.transpose(st[:, b, :], s_sb[g][:, j, P * b : P * b + P], ident_b[:])
+                z_tr = sb.tile([P, 4, P], F32, name="z_tr", tag="z_tr", bufs=2, align_bytes=64)
+                for b in range(4):
+                    nc.scalar.activation(
+                        out=z_tr[:, b, :], in_=st[:, b, :], func=ACT.Identity,
+                        bias=beta_t[:, 4 * h + b : 4 * h + b + 1], scale=1.0,
+                    )
+                z = psum.tile([P, M], F32, name="z_ps", tag="z", bufs=2)
+                for b in range(4):
+                    nc.tensor.transpose(z[:, P * b : P * b + P], z_tr[:, b, :], ident_f[:])
             zt[g, j] = z
 
         def z_max(g, j):
@@ -143,8 +140,8 @@ def tile_masspreconditionedvaluegradientstep_kernel(
         def z_exp(g, j):
             z = zt[g, j]
             nc.scalar.activation(
-                out=e_t[g][:, j, :].rearrange("p (u q e) -> p u q e", u=2, e=2),
-                in_=z[:].rearrange("p (q u e) -> p u q e", u=2, e=2),
+                out=p_t[g][:, j, :].rearrange("p (t q) -> p t q", t=4),
+                in_=z[:].rearrange("p (q t) -> p t q", t=4),
                 func=ACT.Exp,
                 bias=nmax[g][:, j : j + 1],
                 scale=1.0,
@@ -153,31 +150,27 @@ def tile_masspreconditionedvaluegradientstep_kernel(
 
         def recips(g):
             rden[g] = sb.tile([P, 4], F32, name="rden", tag="rden", bufs=3)
-            fac[g] = sb.tile([P, 4], F32, name="fac", tag="fac", bufs=3)
             nc.vector.reciprocal(out=rden[g][:], in_=den[g][:])
-            nc.vector.tensor_tensor(out=fac[g][:], in0=rden[g][:], in1=w_f[:, 4 * g : 4 * g + 4], op=ALU.mult)
+
+        def normalise(g, j):
+            nc.scalar.activation(out=p_t[g][:, j, :], in_=p_t[g][:, j, :], func=ACT.Copy, scale=rden[g][:, j : j + 1])
+
+        pt = {}
+
+        def p_turn(g, j):
+            pt[g, j] = psum.tile([P, 4, P], F32, name="pt", tag="pt", bufs=2)
+            for t in range(4):
+                nc.tensor.transpose(pt[g, j][:, t, :], p_t[g][:, j, P * t : P * t + P], ident_f[:])
 
         def pg_mul(g, j):
             if j == 0:
-                pg[g] = sb.tile([P, 4, M], BF16, name="pg", tag="pg", bufs=2, align_bytes=64)
-            nc.vector.scalar_tensor_tensor(
-                out=pg[g][:, j, :], in0=e_t[g][:, j, :], scalar=rden[g][:, j : j + 1], in1=g_b[:, g // 2, :],
-                op0=ALU.mult, op1=ALU.mult,
-            )
-
-        def pg_turn(g, jp):
-            xt = psum.tile([P, 2, 2, P], F32, name="xt", tag="xt", bufs=1)
-            for jj in range(2):
-                for u in range(2):
-                    nc.tensor.transpose(
-                        xt[:, jj, u, :], pg[g][:, 2 * jp + jj, 256 * u : 256 * u + 256].bitcast(F32), ident_f[:]
-                    )
-            if jp == 0:
                 pgt[g] = sb.tile([P, 4 * P, 4], BF16, name="pgt", tag="pgt", bufs=2, align_bytes=64)
-            dst = pgt[g][:, 256 * jp : 256 * jp + 256, :].rearrange("p n t -> p (n t)").bitcast(F32)
-            nc.scalar.copy(
-                out=dst.rearrange("p (j n u) -> p j n u", j=2, u=2),
-                in_=xt[:].rearrange("p j u n -> p j n u"),
+            h = g // 2
+            nc.vector.tensor_tensor(
+                out=pgt[g][:, P * j : P * j + P, :],
+                in0=pt[g, j][:].rearrange("p t n -> p n t"),
+                in1=gt_f[:, 4 * h : 4 * h + 4].unsqueeze(1).to_broadcast([P, P, 4]),
+                op=ALU.mult,
             )
 
         def quant(src, tag, bufs):
@@ -188,43 +181,34 @@ def tile_masspreconditionedvaluegradientstep_kernel(
             )
             return codes, scales
 
-        def pw_mul(g, u):
-            if u == 0:
+        def pw_mul(g, half):
+            if half == 0:
                 pw[g] = sb.tile([P, M, 4], BF16, name="pw", tag="pw", bufs=2, align_bytes=64)
             nc.vector.tensor_tensor(
-                out=pw[g][:, 256 * u : 256 * u + 256, :].rearrange("p (e q) j -> p q e j", e=2),
-                in0=e_t[g][:, :, 256 * u : 256 * u + 256].rearrange("p j (q e) -> p q e j", e=2),
-                in1=fac[g][:].unsqueeze(1).unsqueeze(1).to_broadcast([P, P, 2, 4]),
+                out=pw[g][:, 256 * half : 256 * half + 256, :].rearrange("p (c i) j -> p c j i", i=2),
+                in0=p_t[g][:, :, 256 * half : 256 * half + 256].rearrange("p j (c i) -> p c j i", i=2),
+                in1=w_f[:, 4 * g : 4 * g + 4].unsqueeze(1).unsqueeze(3).to_broadcast([P, P, 4, 2]),
                 op=ALU.mult,
             )
 
-        cpart = {}
-
-        def mass(g):
-            ps = psum.tile([P, 16], F32, name="cps", tag="xt", bufs=1)
+        def mass(h):
+            cps[h] = psum.tile([P, 4, P], F32, name="cps", tag="cps", bufs=1)
             for t in range(4):
-                u, e = divmod(t, 2)
-                for j in range(4):
+                for k in range(8):
                     nc.tensor.matmul(
-                        out=ps[:, 4 * t + j : 4 * t + j + 1],
-                        lhsT=e_t[g][:, j, 256 * u + e : 256 * u + 256 : 2],
-                        rhs=rden[g][:, j : j + 1],
-                        start=True,
-                        stop=True,
+                        out=cps[h][:, t, :],
+                        lhsT=p_t[2 * h + k // 4][:, k % 4, P * t : P * t + P],
+                        rhs=ident_f[:],
+                        start=(k == 0),
+                        stop=(k == 7),
+                        is_transpose=True,
                     )
-            cps[g] = ps
-
-        def mass_sum(g):
-            cpart[g] = sb.tile([P, 4], F32, name="cpart", tag="cpart", bufs=4)
-            nc.vector.tensor_reduce(
-                out=cpart[g][:], in_=cps[g][:].rearrange("p (t j) -> p t j", t=4), axis=AX.X, op=ALU.add
-            )
 
         def mass_fac(h):
             cs = sb.tile([P, 4], F32, name="cs", tag="cs", bufs=2)
             ch = sb.tile([P, 4], F32, name="ch", tag="ch", bufs=2)
             kf[h] = sb.tile([P, 4], F32, name="kf", tag="kf", bufs=3)
-            nc.vector.tensor_tensor(out=cs[:], in0=cpart[2 * h][:], in1=cpart[2 * h + 1][:], op=ALU.add)
+            nc.vector.tensor_reduce(out=cs[:], in_=cps[h][:], axis=AX.X, op=ALU.add)
             nc.vector.tensor_scalar(out=ch[:], in0=cs[:], scalar1=0.5, scalar2=-0.5, op0=ALU.add, op1=ALU.mult)
             nc.vector.reciprocal(out=kf[h][:], in_=ch[:])
 
@@ -241,9 +225,8 @@ def tile_masspreconditionedvaluegradientstep_kernel(
         def gv_make(h):
             gv[h] = sb.tile([P, 4, D], F32, name="gv", tag="gv", bufs=2, align_bytes=64)
             for t in range(4):
-                nc.gpsimd.tensor_scalar(
-                    out=gv[h][:, t, :], in0=v_sb[h][:, t, :], scalar1=gt_f[:, 4 * h + t : 4 * h + t + 1], scalar2=0.0,
-                    op0=ALU.mult, op1=ALU.add,
+                nc.scalar.activation(
+                    out=gv[h][:, t, :], in_=v_sb[h][:, t, :], func=ACT.Copy, scale=gt_f[:, 4 * h + t : 4 * h + t + 1]
                 )
 
         def mm1(g, j):
@@ -281,7 +264,7 @@ def tile_masspreconditionedvaluegradientstep_kernel(
         def finish(h, t):
             if t == 0:
                 o_t[h] = sb.tile([P, 4, D], F32, name="o_t", tag="o_t", bufs=2, align_bytes=64)
-            gr = psum.tile([P, D], F32, name="gr", tag="gr", bufs=2)
+            gr = psum.tile([P, D], F32, name="gr", tag="gr", bufs=1)
             for gg in range(2):
                 g = 2 * h + gg
                 nc.tensor.matmul_mx(
@@ -321,6 +304,8 @@ def tile_masspreconditionedvaluegradientstep_kernel(
             gz, gp, gm = i + 1, i, i - 1
             has_z, has_p, has_m = gz < G, 0 <= gp < G, 0 <= gm < G
             fh = (i - 3) // 2 if i >= 3 and i % 2 == 1 else None
+            if i >= 0 and i % 2 == 0 and i // 2 + 1 < H:
+                make_bw(i // 2 + 1)
             if i >= 0:
                 if i + 3 < G:
                     load_s(i + 3)
@@ -328,12 +313,12 @@ def tile_masspreconditionedvaluegradientstep_kernel(
                     load_y(i + 2)
                 if i % 2 == 0 and i // 2 + 1 < H:
                     load_v(i // 2 + 1)
-                    make_gb(i // 2 + 1)
-            if has_p:
-                recips(gp)
             if has_z:
-                for j in range(4):
-                    z_make(gz, j)
+                z_make(gz, 0)
+                z_make(gz, 1)
+            if has_p:
+                p_turn(gp, 0)
+                p_turn(gp, 1)
             if has_m:
                 mm1(gm, 0)
                 mm1(gm, 1)
@@ -341,42 +326,48 @@ def tile_masspreconditionedvaluegradientstep_kernel(
                 if has_z:
                     z_max(gz, j)
                     z_exp(gz, j)
+                    if j < 2:
+                        z_make(gz, j + 2)
                 if has_p:
                     pg_mul(gp, j)
+                    if j < 2:
+                        p_turn(gp, j + 2)
                 if has_m and j < 2:
                     mm1(gm, 2 + j)
                 if fh is not None:
                     finish(fh, j)
-                if has_p and j % 2 == 1:
-                    pg_turn(gp, j // 2)
-                if j == 1 and has_m:
-                    mass_sum(gm)
-                    if gm % 2 == 1:
-                        mass_fac(gm // 2)
             if i == -1:
                 v_lay(0)
                 v_quant(0)
+            if i >= 2 and i % 2 == 0:
+                mass(i // 2 - 1)
             if has_p:
                 pw_mul(gp, 0)
+            if has_z:
+                recips(gz)
+            if has_p:
                 pw_mul(gp, 1)
+            if has_p:
+                pgc[gp], pgs[gp] = quant(pgt[gp], "pgq", 2)
             if fh is not None:
                 store(fh)
             if has_m:
                 r_make(gm)
+            if has_z:
+                for j in range(4):
+                    normalise(gz, j)
             if has_p:
-                pgc[gp], pgs[gp] = quant(pgt[gp], "pgq", 2)
-                mass(gp)
                 pwc[gp], pws[gp] = quant(pw[gp], "pwq", 4)
                 for j in range(4):
                     ay_make(gp, j)
+            if i >= 2 and i % 2 == 0:
+                mass_fac(i // 2 - 1)
             if has_m:
                 rc[gm], rs[gm] = quant(r_t[gm], "rq", 4)
             if fh is not None:
                 store_planes(fh)
             if i >= 0 and i % 2 == 1 and (i + 1) // 2 < H:
                 v_lay((i + 1) // 2)
-            if i >= 0 and i % 2 == 0 and i // 2 + 1 < H:
-                make_bw(i // 2 + 1)
             if has_p and gp % 2 == 0:
                 gv_make(gp // 2)
                 if gp > 0:

from contextlib import ExitStack

import concourse.mybir as mybir
from concourse.masks import make_identity

H, N, M, D = 4, 1024, 512, 512
P = 128
G = 2 * H
FLOPS = 2 * 2 * H * N * M * D

F32 = mybir.dt.float32
BF16 = mybir.dt.bfloat16
U32 = mybir.dt.uint32
I32 = mybir.dt.int32
U8 = mybir.dt.uint8
FP8X4 = mybir.dt.float8_e4m3fn_x4
ACT = mybir.ActivationFunctionType
ALU = mybir.AluOpType
AX = mybir.AxisListType


def tile_masspreconditionedvaluegradientstep_kernel(
    tc, s_ref, beta, v_cmp, g_val, y_ref, a_res, w_ref, out_0, out_1, out_2
):
    nc = tc.nc
    with ExitStack() as ctx:
        const = ctx.enter_context(tc.tile_pool(name="const", bufs=1))
        sb = ctx.enter_context(tc.tile_pool(name="sb", bufs=2))
        psum = ctx.enter_context(tc.psum_pool(name="psum", bufs=1))

        s_sb, y_sb, v_sb = {}, {}, {}

        def load_s(g):
            t = sb.tile([P, 4, M], BF16, name="s_sb", tag="s_sb", bufs=5, align_bytes=64)
            h, gg = divmod(g, 2)
            nc.sync.dma_start(out=t[:], in_=s_ref[h, 512 * gg : 512 * gg + 512, :].rearrange("(p j) m -> p j m", j=4))
            s_sb[g] = t

        def load_y(g):
            t = sb.tile([P, 4, D], BF16, name="y_sb", tag="y_sb", bufs=4, align_bytes=64)
            h, gg = divmod(g, 2)
            nc.sync.dma_start(out=t[:], in_=y_ref[h, 512 * gg : 512 * gg + 512, :].rearrange("(p j) d -> p j d", j=4))
            y_sb[g] = t

        def load_v(h):
            t = sb.tile([P, 4, D], BF16, name="v_sb", tag="v_sb", bufs=2, align_bytes=64)
            nc.sync.dma_start(out=t[:], in_=v_cmp[h].rearrange("(p j) d -> p j d", j=4))
            v_sb[h] = t

        warm = const.tile([P, 1], F32, name="warm")
        nc.vector.memset(warm[:], 0.0)
        nc.scalar.activation(out=warm[:], in_=warm[:], func=ACT.Exp)

        load_s(0)
        braw = const.tile([P, P], BF16, name="braw")
        nc.vector.memset(braw[:], 0.0)
        nc.scalar.dma_start(out=braw[0:16, :], in_=beta.rearrange("h (b k) -> (h b) k", k=P))
        a_bf = const.tile([P, H, 2, 4], BF16, name="a_bf")
        w_bf = const.tile([P, H, 2, 4], BF16, name="w_bf")
        gt_bf = const.tile([P, H, 4], BF16, name="gt_bf")
        nc.scalar.dma_start(out=w_bf[:], in_=w_ref.rearrange("h (g p j) -> p h g j", g=2, j=4))
        nc.scalar.dma_start(out=a_bf[:], in_=a_res.rearrange("h (g p j) -> p h g j", g=2, j=4))
        nc.scalar.dma_start(out=gt_bf[:], in_=g_val.rearrange("h (p t) -> p h t", t=4))
        load_v(0)
        load_s(1)
        load_y(0)
        load_s(2)
        load_y(1)

        ident_b = const.tile([P, P], BF16, name="ident_b")
        make_identity(nc, ident_b[:])
        ident_f = const.tile([P, P], F32, name="ident_f")
        make_identity(nc, ident_f[:])

        bt_ps = psum.tile([P, P], BF16, name="bt_ps", tag="cps", bufs=1)
        nc.tensor.transpose(bt_ps[:], braw[:], ident_b[:])
        beta_t = const.tile([P, 16], F32, name="beta_t")
        nc.vector.tensor_copy(out=beta_t[:], in_=bt_ps[:, 0:16])
        a_f = const.tile([P, 32], F32, name="a_f")
        nc.vector.tensor_copy(out=a_f[:], in_=a_bf[:].rearrange("p h g j -> p (h g j)"))
        w_f = const.tile([P, 32], F32, name="w_f")
        nc.vector.tensor_copy(out=w_f[:], in_=w_bf[:].rearrange("p h g j -> p (h g j)"))
        gt_f = const.tile([P, 16], F32, name="gt_f")
        nc.vector.tensor_copy(out=gt_f[:], in_=gt_bf[:].rearrange("p h t -> p (h t)"))
        beta_w = {}

        def make_bw(h):
            beta_w[h] = sb.tile([P, 4, P], F32, name="beta_w", tag="beta_w", bufs=2, align_bytes=64)
            nc.vector.tensor_copy(
                out=beta_w[h][:], in_=beta_t[:, 4 * h : 4 * h + 4].unsqueeze(2).to_broadcast([P, 4, P])
            )

        make_bw(0)

        p_t, nmax, den, rden = {}, {}, {}, {}
        pgt, pgc, pgs = {}, {}, {}
        pw, pwc, pws = {}, {}, {}
        u_t, ay_t, r_t, rc, rs = {}, {}, {}, {}, {}
        vb, vc, vs, gv, kf, cps = {}, {}, {}, {}, {}, {}
        o_t, ob, oc, osc = {}, {}, {}, {}

        zt = {}

        def z_make(g, j):
            h = g // 2
            if j == 0:
                p_t[g] = sb.tile([P, 4, M], F32, name="p_t", tag="p_t", bufs=4, align_bytes=64)
                nmax[g] = sb.tile([P, 4], F32, name="nmax", tag="nmax", bufs=3)
                den[g] = sb.tile([P, 4], F32, name="den", tag="den", bufs=3)
            if j < 3:
                z = psum.tile([P, M], F32, name="z_ps", tag="z", bufs=2)
                nc.tensor.matmul(out=z[:], lhsT=ident_b[:], rhs=s_sb[g][:, j, :], start=True, stop=False)
                for b in range(4):
                    nc.tensor.matmul(
                        out=z[:, P * b : P * b + P],
                        lhsT=beta_w[h][:, b, :],
                        rhs=ident_f[:],
                        start=False,
                        stop=(b == 3),
                        is_transpose=True,
                    )
            else:
                st = psum.tile([P, 4, P], BF16, name="st_ps", tag="z", bufs=2)
                for b in range(4):
                    nc.tensor.transpose(st[:, b, :], s_sb[g][:, j, P * b : P * b + P], ident_b[:])
                z_tr = sb.tile([P, 4, P], F32, name="z_tr", tag="z_tr", bufs=2, align_bytes=64)
                for b in range(4):
                    nc.scalar.activation(
                        out=z_tr[:, b, :], in_=st[:, b, :], func=ACT.Identity,
                        bias=beta_t[:, 4 * h + b : 4 * h + b + 1], scale=1.0,
                    )
                z = psum.tile([P, M], F32, name="z_ps", tag="z", bufs=2)
                for b in range(4):
                    nc.tensor.transpose(z[:, P * b : P * b + P], z_tr[:, b, :], ident_f[:])
            zt[g, j] = z

        def z_max(g, j):
            nc.vector.tensor_reduce(out=nmax[g][:, j : j + 1], in_=zt[g, j][:], axis=AX.X, op=ALU.max, negate=True)

        def z_exp(g, j):
            z = zt[g, j]
            nc.scalar.activation(
                out=p_t[g][:, j, :].rearrange("p (t q) -> p t q", t=4),
                in_=z[:].rearrange("p (q t) -> p t q", t=4),
                func=ACT.Exp,
                bias=nmax[g][:, j : j + 1],
                scale=1.0,
                accum_out=den[g][:, j : j + 1],
            )

        def recips(g):
            rden[g] = sb.tile([P, 4], F32, name="rden", tag="rden", bufs=3)
            nc.vector.reciprocal(out=rden[g][:], in_=den[g][:])

        def normalise(g, j):
            nc.scalar.activation(out=p_t[g][:, j, :], in_=p_t[g][:, j, :], func=ACT.Copy, scale=rden[g][:, j : j + 1])

        pt = {}

        def p_turn(g, j):
            pt[g, j] = psum.tile([P, 4, P], F32, name="pt", tag="pt", bufs=2)
            for t in range(4):
                nc.tensor.transpose(pt[g, j][:, t, :], p_t[g][:, j, P * t : P * t + P], ident_f[:])

        def pg_mul(g, j):
            if j == 0:
                pgt[g] = sb.tile([P, 4 * P, 4], BF16, name="pgt", tag="pgt", bufs=2, align_bytes=64)
            h = g // 2
            nc.vector.tensor_tensor(
                out=pgt[g][:, P * j : P * j + P, :],
                in0=pt[g, j][:].rearrange("p t n -> p n t"),
                in1=gt_f[:, 4 * h : 4 * h + 4].unsqueeze(1).to_broadcast([P, P, 4]),
                op=ALU.mult,
            )

        def quant(src, tag, bufs):
            codes = sb.tile([P, 512], U32, name=tag + "_c", tag=tag + "_c", bufs=bufs, align_bytes=64)
            scales = sb.tile([P, 512], U8, name=tag + "_s", tag=tag + "_s", bufs=bufs, align_bytes=64)
            nc.vector.quantize_mx(
                out=codes[:].bitcast(FP8X4), scales=scales[:], in_=src[:].rearrange("p c j -> p (c j)")
            )
            return codes, scales

        def pw_mul(g, half):
            if half == 0:
                pw[g] = sb.tile([P, M, 4], BF16, name="pw", tag="pw", bufs=2, align_bytes=64)
            nc.vector.tensor_tensor(
                out=pw[g][:, 256 * half : 256 * half + 256, :].rearrange("p (c i) j -> p c j i", i=2),
                in0=p_t[g][:, :, 256 * half : 256 * half + 256].rearrange("p j (c i) -> p c j i", i=2),
                in1=w_f[:, 4 * g : 4 * g + 4].unsqueeze(1).unsqueeze(3).to_broadcast([P, P, 4, 2]),
                op=ALU.mult,
            )

        def mass(h):
            cps[h] = psum.tile([P, 4, P], F32, name="cps", tag="cps", bufs=1)
            for t in range(4):
                for k in range(8):
                    nc.tensor.matmul(
                        out=cps[h][:, t, :],
                        lhsT=p_t[2 * h + k // 4][:, k % 4, P * t : P * t + P],
                        rhs=ident_f[:],
                        start=(k == 0),
                        stop=(k == 7),
                        is_transpose=True,
                    )

        def mass_fac(h):
            cs = sb.tile([P, 4], F32, name="cs", tag="cs", bufs=2)
            ch = sb.tile([P, 4], F32, name="ch", tag="ch", bufs=2)
            kf[h] = sb.tile([P, 4], F32, name="kf", tag="kf", bufs=3)
            nc.vector.tensor_reduce(out=cs[:], in_=cps[h][:], axis=AX.X, op=ALU.add)
            nc.vector.tensor_scalar(out=ch[:], in0=cs[:], scalar1=0.5, scalar2=-0.5, op0=ALU.add, op1=ALU.mult)
            nc.vector.reciprocal(out=kf[h][:], in_=ch[:])

        def v_lay(h):
            vb[h] = sb.tile([P, D, 4], BF16, name="vb", tag="vb", bufs=2, align_bytes=64)
            nc.scalar.copy(
                out=vb[h][:].rearrange("p (c i) j -> p c j i", i=4),
                in_=v_sb[h][:].rearrange("p j (c i) -> p c j i", i=4),
            )

        def v_quant(h):
            vc[h], vs[h] = quant(vb[h], "vq", 2)

        def gv_make(h):
            gv[h] = sb.tile([P, 4, D], F32, name="gv", tag="gv", bufs=2, align_bytes=64)
            for t in range(4):
                nc.scalar.activation(
                    out=gv[h][:, t, :], in_=v_sb[h][:, t, :], func=ACT.Copy, scale=gt_f[:, 4 * h + t : 4 * h + t + 1]
                )

        def mm1(g, j):
            h = g // 2
            acc = psum.tile([P, D], F32, name="acc", tag="acc", bufs=2)
            nc.tensor.matmul_mx(
                out=acc[:],
                lhsT=pgc[g][:, P * j : P * j + P].bitcast(FP8X4),
                lhsT_scale=pgs[g][:, P * j : P * j + P],
                rhs=vc[h][:].bitcast(FP8X4),
                rhs_scale=vs[h][:],
                start=True,
                stop=True,
            )
            if j == 0:
                u_t[g] = sb.tile([P, 4, D], F32, name="u_t", tag="u_t", bufs=2, align_bytes=64)
            nc.scalar.activation(out=u_t[g][:, j, :], in_=acc[:], func=ACT.Copy, scale=a_f[:, 4 * g + j : 4 * g + j + 1])

        def ay_make(g, j):
            if j == 0:
                ay_t[g] = sb.tile([P, 4, D], F32, name="ay_t", tag="ay_t", bufs=2, align_bytes=64)
            nc.scalar.activation(
                out=ay_t[g][:, j, :], in_=y_sb[g][:, j, :], func=ACT.Copy, scale=a_f[:, 4 * g + j : 4 * g + j + 1]
            )

        def r_make(g):
            r_t[g] = sb.tile([P, D, 4], BF16, name="r_t", tag="r_t", bufs=2, align_bytes=64)
            nc.vector.tensor_tensor(
                out=r_t[g][:].rearrange("p (c i) j -> p c j i", i=2),
                in0=u_t[g][:].rearrange("p j (c i) -> p c j i", i=2),
                in1=ay_t[g][:].rearrange("p j (c i) -> p c j i", i=2),
                op=ALU.subtract,
            )

        def finish(h, t):
            if t == 0:
                o_t[h] = sb.tile([P, 4, D], F32, name="o_t", tag="o_t", bufs=2, align_bytes=64)
            gr = psum.tile([P, D], F32, name="gr", tag="gr", bufs=1)
            for gg in range(2):
                g = 2 * h + gg
                nc.tensor.matmul_mx(
                    out=gr[:],
                    lhsT=pwc[g][:, P * t : P * t + P].bitcast(FP8X4),
                    lhsT_scale=pws[g][:, P * t : P * t + P],
                    rhs=rc[g][:].bitcast(FP8X4),
                    rhs_scale=rs[g][:],
                    start=(gg == 0),
                    stop=(gg == 1),
                )
            nc.vector.scalar_tensor_tensor(
                out=o_t[h][:, t, :], in0=gr[:], scalar=kf[h][:, t : t + 1], in1=gv[h][:, t, :], op0=ALU.mult, op1=ALU.add
            )

        def store(h):
            nc.sync.dma_start(out=out_0[h].rearrange("(p t) d -> p t d", t=4), in_=o_t[h][:])
            ob[h] = sb.tile([P, D, 4], BF16, name="ob", tag="ob", bufs=2, align_bytes=64)
            nc.scalar.copy(
                out=ob[h][:].rearrange("p (c i) t -> p c t i", i=2),
                in_=o_t[h][:].rearrange("p t (c i) -> p c t i", i=2),
            )

        def store_planes(h):
            oc[h], osc[h] = quant(ob[h], "oq", 2)
            cols = slice(D * h, D * h + D)
            nc.sync.dma_start(
                out=out_1[0, :, cols, :].rearrange("p m t -> p (m t)").bitcast(I32), in_=oc[h][:].bitcast(I32)
            )
            for qq in range(4):
                nc.sync.dma_start(
                    out=out_2[0, 4 * qq : 4 * qq + 4, cols].bitcast(I32),
                    in_=osc[h][32 * qq : 32 * qq + 4, :].bitcast(I32),
                )

        for i in range(-1, G + 2):
            gz, gp, gm = i + 1, i, i - 1
            has_z, has_p, has_m = gz < G, 0 <= gp < G, 0 <= gm < G
            fh = (i - 3) // 2 if i >= 3 and i % 2 == 1 else None
            if i >= 0 and i % 2 == 0 and i // 2 + 1 < H:
                make_bw(i // 2 + 1)
            if i >= 0:
                if i + 3 < G:
                    load_s(i + 3)
                if i + 2 < G:
                    load_y(i + 2)
                if i % 2 == 0 and i // 2 + 1 < H:
                    load_v(i // 2 + 1)
            if has_z:
                z_make(gz, 0)
                z_make(gz, 1)
            if has_p:
                p_turn(gp, 0)
                p_turn(gp, 1)
            if has_m:
                mm1(gm, 0)
                mm1(gm, 1)
            for j in range(4):
                if has_z:
                    z_max(gz, j)
                    z_exp(gz, j)
                    if j < 2:
                        z_make(gz, j + 2)
                if has_p:
                    pg_mul(gp, j)
                    if j < 2:
                        p_turn(gp, j + 2)
                if has_m and j < 2:
                    mm1(gm, 2 + j)
                if fh is not None:
                    finish(fh, j)
            if i == -1:
                v_lay(0)
                v_quant(0)
            if i >= 2 and i % 2 == 0:
                mass(i // 2 - 1)
            if has_p:
                pw_mul(gp, 0)
            if has_z:
                recips(gz)
            if has_p:
                pw_mul(gp, 1)
            if has_p:
                pgc[gp], pgs[gp] = quant(pgt[gp], "pgq", 2)
            if fh is not None:
                store(fh)
            if has_m:
                r_make(gm)
            if has_z:
                for j in range(4):
                    normalise(gz, j)
            if has_p:
                pwc[gp], pws[gp] = quant(pw[gp], "pwq", 4)
                for j in range(4):
                    ay_make(gp, j)
            if i >= 2 and i % 2 == 0:
                mass_fac(i // 2 - 1)
            if has_m:
                rc[gm], rs[gm] = quant(r_t[gm], "rq", 4)
            if fh is not None:
                store_planes(fh)
            if i >= 0 and i % 2 == 1 and (i + 1) // 2 < H:
                v_lay((i + 1) // 2)
            if has_p and gp % 2 == 0:
                gv_make(gp // 2)
                if gp > 0:
                    v_quant(gp // 2)
